import numpy as np
import ml_dtypes


def mxq(x, axis, fmt="e4m3"):
    dtype, down = {"e4m3": (ml_dtypes.float8_e4m3fn, 7), "e5m2": (ml_dtypes.float8_e5m2, 14)}[fmt]
    v = np.moveaxis(np.asarray(x, np.float32).astype(ml_dtypes.bfloat16).astype(np.float64), axis, -1)
    blocks = v.reshape(v.shape[:-1] + (-1, 32))
    amax = np.abs(blocks).max(-1, keepdims=True)
    byte = np.maximum(np.where(amax > 0, np.frexp(amax)[1] - 1 + 127, 0) - down, 1)
    scale = np.exp2(byte - 127.0)
    codes = (blocks / scale).astype(np.float32).astype(dtype).astype(np.float64)
    return np.moveaxis((codes * scale).reshape(v.shape), -1, axis)


WIDE = False


def mx_kscale(k):
    if not WIDE:
        return np.ones(k)
    levels = np.array([10, -10, 5, -5, 0])
    if k % 512:
        return np.exp2(np.random.permutation(np.resize(levels, k // 32))).repeat(32)
    a = np.empty((k // 512, 16))
    for p in range(k // 512):
        a[p, :8] = np.random.permutation(np.resize(levels, 8))
        for g in range(8):
            far = levels[np.abs(levels - a[p, g]) >= 10]
            a[p, g + 8] = far[np.random.randint(len(far))]
    return np.exp2(a.ravel()).repeat(32)


def f64(x):
    return np.asarray(x).astype(np.float64)


def striped(idx):
    return np.tile(idx.reshape(-1, 16).T, (8, 1)).astype(np.uint16)


def unstriped(offs):
    return offs[:16].T.reshape(-1).astype(np.int64)


def striped8(idx):
    return np.concatenate([x.reshape(-1, 16).T for x in idx]).astype(np.uint16)


def runs(offs, k):
    lists = np.stack([offs[16 * r : 16 * r + 16].T.reshape(-1) for r in range(8)]).astype(np.int64)
    return lists[np.arange(k) % 512 // 64]


def pack_weight(w):
    k, n = w.shape
    w = f64(np.asarray(w, np.float32).astype(ml_dtypes.bfloat16)).reshape(k // 32, 32, n)
    amax = np.abs(w).max(1)
    byte = np.clip(np.where(amax > 0, np.frexp(amax)[1] - 1 + 127 - 7, 1), 1, 254)
    scaled = (w * np.exp2(127.0 - byte)[:, None, :]).reshape(k, n).astype(np.float32)
    words = np.ascontiguousarray(scaled.reshape(k // 512, 128, 4, n).transpose(0, 1, 3, 2)).astype(ml_dtypes.float8_e4m3fn).view(np.uint8)
    return words, np.ascontiguousarray(byte.astype(np.uint8).reshape(k // 512, 16, n))


def unpack_weight(words, scales):
    g, p, n, _ = words.shape
    vals = np.ascontiguousarray(words).view(ml_dtypes.float8_e4m3fn).astype(np.float64) * np.repeat(np.exp2(scales.astype(np.float64) - 127.0), 8, axis=1)[..., None]
    return vals.transpose(0, 1, 3, 2).reshape(g * 512, n)

def planes(y):
    n, m = y.shape
    v = y.astype(np.float32).astype(ml_dtypes.bfloat16).astype(np.float64).reshape(n // 32, 32, m)
    top = np.abs(v).max(1)
    byte = np.clip(np.where(top > 0, np.frexp(top)[1] - 1 + 127 - 7, 1), 1, 254)
    codes = (v * np.exp2(127.0 - byte)[:, None, :]).reshape(n, m).astype(np.float32).astype(ml_dtypes.float8_e4m3fn).view(np.uint8)
    words = codes.reshape(n // 512, 128, 4, m).transpose(0, 1, 3, 2)
    return np.ascontiguousarray(words), np.ascontiguousarray(byte.astype(np.uint8).reshape(n // 512, 16, m))


K, T, S, G, H, W, C, U = 512, 1024, 512, 2048, 512, 256, 512, 1024


def setup_inputs():
    n = np.random.standard_normal
    s = mx_kscale(K)[:, None]
    packed_xT = pack_weight(n((K, T)) * s)
    packed_dT = pack_weight(n((K, G)) / s)
    perm = np.random.permutation(S)
    perm2 = np.random.permutation(S)
    perm3 = np.stack([np.random.permutation(U) for _ in range(8)])
    return {
        "x_words": packed_xT[0],
        "x_scales": packed_xT[1],
        "d_words": packed_dT[0],
        "d_scales": packed_dT[1],
        "gs": (np.random.uniform(0.5, 1.5, (K, 1)) / s).astype(np.float32),
        "offs": striped(np.random.permutation(T)[:S]),
        "k1": striped8(np.random.randint(0, G, (8, H))),
        "two": striped(np.random.permutation(T)[:S]),
        "k2": striped8(np.random.randint(0, G, (8, H))),
        "hz": striped8(np.random.randint(0, T, (8, S))),
        "k3": striped8(np.random.randint(0, G, (8, H))),
        "n1": striped(perm[:W]),
        "n2": striped(perm[W:]),
        "n3": striped(perm2[:W]),
        "n4": striped(perm2[W:]),
        "n5": striped(np.random.permutation(S)),
        "cand": striped8(np.random.randint(0, T, (8, C))),
        "n6": striped8(perm3[:, :S]),
        "n7": striped8(perm3[:, S:]),
        "n8": striped8(np.stack([np.random.permutation(S) for _ in range(8)])),
    }


def reference(x_words, x_scales, d_words, d_scales, gs, offs, k1, two, k2, hz, k3, n1, n2, n3, n4, n5, cand, n6, n7, n8):
    x_cand = unpack_weight(x_words, x_scales)[np.arange(K)[:, None], runs(cand, K)]
    d_k1 = unpack_weight(d_words, d_scales)[np.arange(K)[:, None], runs(k1, K)]
    xq = unpack_weight(x_words, x_scales)[:, unstriped(offs)]
    d_k2 = unpack_weight(d_words, d_scales)[np.arange(K)[:, None], runs(k2, K)]
    x_two = unpack_weight(x_words, x_scales)[:, unstriped(two)]
    d_k3 = unpack_weight(d_words, d_scales)[np.arange(K)[:, None], runs(k3, K)]
    x_hz = unpack_weight(x_words, x_scales)[np.arange(K)[:, None], runs(hz, K)]
    h = 0.0625 * (d_k1.T @ xq + d_k2.T @ x_two + d_k3.T @ x_hz)
    pa = h[:, unstriped(n1)]
    pb = h[:, unstriped(n2)]
    rb = np.maximum(pa, pb)
    ua = np.zeros((H, S))
    ua[:, unstriped(n3)] = pb
    ub = ua.copy()
    ub[:, unstriped(n4)] = rb
    z = f64(gs) * (ub - h[:, unstriped(n5)])
    s = 0.0625 * ((x_cand.T @ mxq(z, 0, "e4m3")))
    ds = np.zeros((C, S))
    ds[np.arange(C)[:, None], runs(n8, C)] = s
    up = np.maximum(s, ds)
    ph = np.zeros((C, U))
    ph[np.arange(C)[:, None], runs(n6, C)] = ds
    out = ph.copy()
    out[np.arange(C)[:, None], runs(n7, C)] = up
    return (out,) + planes(out)

@@ -1,0 +1,315 @@
+from contextlib import ExitStack
+
+import concourse.mybir as mybir
+
+F32 = mybir.dt.float32
+BF16 = mybir.dt.bfloat16
+I32 = mybir.dt.int32
+U32 = mybir.dt.uint32
+U16 = mybir.dt.uint16
+U8 = mybir.dt.uint8
+FP8X4 = mybir.dt.float8_e4m3fn_x4
+COPY = mybir.ActivationFunctionType.Copy
+ALU = mybir.AluOpType
+
+P = 128
+PACK = 4
+T, G, S, W, U = 1024, 2048, 512, 256, 1024
+SIXTEENTH = 0.0625
+FLOPS = 4 * 2 * 512 * 512 * 512
+
+
+def tile_picked_mtthzkcpswpagsn_none_po_kernel(
+    tc, x_words, x_scales, d_words, d_scales, gs, offs, k1, two, k2, hz, k3,
+    n1, n2, n3, n4, n5, cand, n6, n7, n8, out_0, out_1, out_2,
+):
+    nc = tc.nc
+    with ExitStack() as ctx:
+        lists = ctx.enter_context(tc.tile_pool(name="lists", bufs=1))
+        pool = ctx.enter_context(tc.tile_pool(name="work", bufs=1))
+        shared = ctx.enter_context(tc.tile_pool(name="shared", bufs=1))
+        psum = ctx.enter_context(tc.psum_pool(name="psum", bufs=1))
+
+        def sb(name, shape, dtype, tag=None):
+            return pool.tile(shape, dtype, name=name, tag=tag or name, align_bytes=64)
+
+        def load_list(name, dram):
+            held = lists.tile(list(dram.shape), U16, name=name, tag=name)
+            nc.sync.dma_start(held[:], dram)
+            return held
+
+        def load_scale_rows(name, dram, columns):
+            window = sb(name, [P, columns], U8)
+            nc.gpsimd.memset(window[:].bitcast(I32), 0)
+            nc.sync.dma_start(window[:].bitcast(I32)[0:P:8, :], dram[0].bitcast(I32))
+            return window
+
+        def load_words(name, dram, columns):
+            window = sb(name, [P, columns], U32)
+            nc.sync.dma_start(
+                window[:].bitcast(I32), dram[0].rearrange("p n t -> p (n t)").bitcast(I32)
+            )
+            return window
+
+        def gather(out, window, offsets):
+            nc.vector.tensor_copy(out, window[:].indirect(offsets))
+
+        def place_scale_rows(planes, first_row, picked, columns, queues):
+            for q in range(4):
+                queues[q % len(queues)].dma_start(
+                    planes[:].bitcast(I32)[32 * q + first_row : 32 * q + first_row + 4, 0 : columns // 4],
+                    picked[:].bitcast(I32)[32 * q : 32 * q + 32 : 8, :],
+                )
+
+        def deal_words(name, picked):
+            dealt = sb(name, [P, S], U32)
+            nc.vector.tensor_copy(
+                dealt[:].bitcast(I32).rearrange("p (t a b) -> p a t b", t=PACK, b=4),
+                picked[:].bitcast(I32).rearrange("p (a b t) -> p a t b", t=PACK, b=4),
+            )
+            return dealt
+
+        def deal_bytes(name, planes):
+            dealt = sb(name, [P, S], U8)
+            nc.vector.tensor_copy(
+                dealt[:].rearrange("p (t m) -> p t m", t=PACK),
+                planes[:, 0:S].rearrange("p (m t) -> p t m", t=PACK),
+            )
+            return dealt
+
+        x_w = load_words("x_w", x_words, T)
+        x_sc = load_scale_rows("x_sc", x_scales, T)
+        d_sc = load_scale_rows("d_sc", d_scales, G)
+        offs_l = load_list("offs", offs)
+        two_l = load_list("two", two)
+        hz_l = load_list("hz", hz)
+        k1_l = load_list("k1", k1)
+        k2_l = load_list("k2", k2)
+        k3_l = load_list("k3", k3)
+        d_w = load_words("d_w", d_words, G)
+        cand_l = load_list("cand", cand)
+        n2_l = load_list("n2", n2)
+        n1_l = load_list("n1", n1)
+        n3_l = load_list("n3", n3)
+        n4_l = load_list("n4", n4)
+        n5_l = load_list("n5", n5)
+        gs_sb = sb("gs", [P, PACK], F32)
+        nc.sync.dma_start(gs_sb[:], gs.rearrange("(p t) o -> p (t o)", t=PACK))
+        n8_l = load_list("n8", n8)
+        n6_l = load_list("n6", n6)
+        n7_l = load_list("n7", n7)
+
+        planes = sb("planes", [P, 4 * S], U8)
+        nc.vector.memset(planes[:].bitcast(I32), 0)
+        cand_plane = sb("cand_plane", [P, S], U8)
+        nc.vector.memset(cand_plane[:].bitcast(I32), 0)
+
+        mov = []
+        for j, held in enumerate((offs_l, two_l)):
+            picked = sb("xw%d" % j, [P, S], U32)
+            gather(picked[:], x_w, held[:])
+            mov.append(picked)
+
+        picked4 = sb("picked4", [P, 4 * S], U8)
+        for j, window, held in ((1, x_sc, offs_l), (2, x_sc, two_l), (3, x_sc, hz_l), (0, d_sc, k1_l)):
+            gather(picked4[:, j * S : (j + 1) * S], window, held[:])
+        place_scale_rows(planes, 0, picked4, 4 * S, (nc.sync, nc.scalar))
+        picked_k2 = sb("picked_k2", [P, S], U8)
+        gather(picked_k2[:], d_sc, k2_l[:])
+        place_scale_rows(planes, 4, picked_k2, S, (nc.sync, nc.scalar))
+        picked_k3 = shared.tile([P, S], U8, name="picked_k3", tag="picked_k3", align_bytes=64, offset=4 * S - S // 2)
+        gather(picked_k3[:], d_sc, k3_l[:])
+        place_scale_rows(planes, 8, picked_k3, S, (nc.sync, nc.scalar))
+
+        dealt = []
+        for j, held in enumerate((k1_l, k2_l, k3_l)):
+            picked = sb("kw%d" % j, [P, S], U32)
+            gather(picked[:], d_w, held[:])
+            if j > 0:
+                dealt.append(deal_words("kd%d" % (j - 1), before))
+            before = picked
+        dealt.append(deal_words("kd2", before))
+        stat_scales = deal_bytes("stat_scales", planes)
+        picked = shared.tile([P, S], U32, name="xw2", tag="xw2", align_bytes=64, offset=0)
+        gather(picked[:], x_w, hz_l[:])
+        mov.append(picked)
+
+        banks = [psum.tile([P, S], F32, name="hb%d" % t, tag="bank%d" % t) for t in range(PACK)]
+        for t in range(PACK):
+            for j in range(3):
+                cols = slice(t * P, (t + 1) * P)
+                nc.tensor.matmul_mx(
+                    out=banks[t][:],
+                    lhsT=dealt[j][:, cols].bitcast(FP8X4),
+                    lhsT_scale=stat_scales[4 * j : P, cols],
+                    rhs=mov[j][:].bitcast(FP8X4),
+                    rhs_scale=planes[:, (j + 1) * S : (j + 2) * S],
+                    start=(j == 0),
+                    stop=(j == 2),
+                )
+
+        picked_c = shared.tile([P, S], U8, name="picked_c", tag="picked_c", align_bytes=64, offset=4 * S)
+        gather(picked_c[:], x_sc, cand_l[:])
+        place_scale_rows(cand_plane, 0, picked_c, S, (nc.sync,))
+
+        HALF = S // 2
+        zb = [sb("zb%d" % c, [P, HALF, PACK], BF16) for c in range(2)]
+        h, pa, pb, ub, h5, diff = [], [], [], [], [], []
+
+        def fetch_pairs(t):
+            h.append(sb("h%d" % t, [P, S], F32))
+            nc.scalar.activation(h[t][:], banks[t][:], COPY, scale=SIXTEENTH)
+            pb.append(sb("pb%d" % t, [P, W], F32))
+            nc.scalar.activation(pb[t][:], h[t][:].indirect(n2_l[:]), COPY)
+            pa.append(sb("pa%d" % t, [P, W], F32))
+            nc.scalar.activation(pa[t][:], h[t][:].indirect(n1_l[:]), COPY)
+
+        def put_pairs(t):
+            ub.append(sb("ub%d" % t, [P, S], F32))
+            nc.vector.tensor_copy(ub[t][:].indirect(n3_l[:]), pb[t][:])
+            rb = sb("rb%d" % t, [P, W], F32)
+            nc.vector.tensor_tensor(rb[:], pa[t][:], pb[t][:], ALU.max)
+            nc.vector.tensor_copy(ub[t][:].indirect(n4_l[:]), rb[:])
+
+        def fetch_n5(t):
+            h5.append(sb("h5_%d" % t, [P, S], F32))
+            for c in range(2):
+                nc.scalar.activation(
+                    h5[t][:, c * HALF : (c + 1) * HALF],
+                    h[t][:].indirect(n5_l[:, c * 16 : (c + 1) * 16]),
+                    COPY,
+                )
+
+        def subtract(t):
+            diff.append(sb("diff%d" % t, [P, S], F32))
+            nc.vector.tensor_tensor(diff[t][:], ub[t][:], h5[t][:], ALU.subtract)
+
+        def round_z(t):
+            for c in range(2):
+                nc.scalar.activation(
+                    zb[c][:, :, t], diff[t][:, c * HALF : (c + 1) * HALF], COPY, scale=gs_sb[:, t : t + 1]
+                )
+
+        fetch_pairs(0)
+        put_pairs(0)
+        fetch_pairs(1)
+        fetch_n5(0)
+        put_pairs(1)
+        subtract(0)
+        fetch_pairs(2)
+        fetch_n5(1)
+        put_pairs(2)
+        subtract(1)
+        fetch_pairs(3)
+        round_z(0)
+        fetch_n5(2)
+        cand_scales = deal_bytes("cand_scales", cand_plane)
+        put_pairs(3)
+        subtract(2)
+        fetch_n5(3)
+        round_z(1)
+        round_z(2)
+        subtract(3)
+        round_z(3)
+
+        picked_cw = sb("picked_cw", [P, S], U32, tag="ub3")
+        gather(picked_cw[:], x_w, cand_l[:])
+        cand_words = deal_words("cand_words", picked_cw)
+
+        z_words = sb("z_words", [P, S], U32)
+        z_scales = sb("z_scales", [P, S], U8)
+        for c in range(2):
+            cols = slice(c * HALF, (c + 1) * HALF)
+            nc.vector.quantize_mx(
+                out=z_words[:, cols].bitcast(FP8X4),
+                scales=z_scales[:, cols],
+                in_=zb[c][:].rearrange("p n t -> p (n t)"),
+            )
+
+        s = [sb("s%d" % t, [P, S], F32) for t in range(PACK)]
+
+        def score(t, cols, tag):
+            width = cols.stop - cols.start
+            bank = psum.tile([P, width], F32, name="sb_" + tag, tag=tag)
+            rows = slice(t * P, (t + 1) * P)
+            nc.tensor.matmul_mx(
+                out=bank[:],
+                lhsT=cand_words[:, rows].bitcast(FP8X4),
+                lhsT_scale=cand_scales[:, rows],
+                rhs=z_words[:, cols].bitcast(FP8X4),
+                rhs_scale=z_scales[:, cols],
+                start=True,
+                stop=True,
+            )
+            nc.scalar.activation(s[t][:, cols], bank[:], COPY, scale=SIXTEENTH)
+
+        score(2, slice(0, HALF), "bank4")
+        score(2, slice(HALF, S), "bank5")
+        score(0, slice(0, S), "bank6")
+        score(1, slice(0, S), "bank7")
+        score(3, slice(0, S), "bank0")
+
+        CH = 256
+        ob = [sb("ob%d" % c, [P, CH, PACK], BF16) for c in range(U // CH)]
+        out_rows = out_0.rearrange("(p t) n -> t p n", t=PACK)
+        ds, up, page = {}, {}, {}
+
+        def send(t):
+            ds[t] = sb("ds%d" % t, [P, 2 * S], F32)
+            if t == 2:
+                for c in range(2):
+                    nc.vector.tensor_copy(
+                        ds[t][:].indirect(n8_l[:, c * 16 : (c + 1) * 16]), s[t][:, c * HALF : (c + 1) * HALF]
+                    )
+            else:
+                nc.vector.tensor_copy(ds[t][:].indirect(n8_l[:]), s[t][:])
+
+        def larger(t):
+            up[t] = sb("up%d" % t, [P, S], F32)
+            nc.vector.tensor_tensor(up[t][:], s[t][:], ds[t][:, 0:S], ALU.max)
+
+        def put_ds(t):
+            page[t] = sb("page%d" % t, [P, U], F32, tag="page%d" % (t % 2 if t < 2 else 2))
+            nc.vector.tensor_copy(page[t][:].indirect(n6_l[:]), ds[t][:, 0:S])
+
+        def put_up(t):
+            nc.vector.tensor_copy(page[t][:].indirect(n7_l[:]), up[t][:])
+            nc.sync.dma_start(out_rows[t], page[t][:])
+            for c in range(U // CH):
+                if t == 3 and c < 2:
+                    nc.vector.tensor_copy(ob[c][:, :, t], page[t][:, c * CH : (c + 1) * CH])
+                else:
+                    nc.scalar.copy(ob[c][:, :, t], page[t][:, c * CH : (c + 1) * CH])
+
+        send(2)
+        send(0)
+        larger(2)
+        put_ds(2)
+        send(1)
+        put_up(2)
+        larger(0)
+        put_ds(0)
+        send(3)
+        put_up(0)
+        larger(1)
+        put_ds(1)
+        larger(3)
+        put_up(1)
+        put_ds(3)
+        put_up(3)
+
+        o_words = sb("o_words", [P, U], U32)
+        o_scales = sb("o_scales", [P, U], U8)
+        words_out = out_1[0].rearrange("p n t -> p (n t)").bitcast(I32)
+        for c in range(U // CH):
+            cols = slice(c * CH, (c + 1) * CH)
+            nc.vector.quantize_mx(
+                out=o_words[:, cols].bitcast(FP8X4),
+                scales=o_scales[:, cols],
+                in_=ob[c][:].rearrange("p n t -> p (n t)"),
+            )
+            nc.sync.dma_start(words_out[:, cols], o_words[:].bitcast(I32)[:, cols])
+        for q in range(4):
+            nc.sync.dma_start(
+                out_2[0].bitcast(I32)[4 * q : 4 * q + 4, :], o_scales[:].bitcast(I32)[32 * q : 32 * q + 4, :]
+            )

@@ -54,30 +54,29 @@ def tile_picked_mtthzkcpswpagsn_none_po_kernel(
         def gather(out, window, offsets):
             nc.vector.tensor_copy(out, window[:].indirect(offsets))
 
-        def place_scale_rows(planes, first_row, picked, columns, queues):
+        def place_scale_rows(planes, first_row, picked, start, columns, queues):
             for q in range(4):
                 queues[q % len(queues)].dma_start(
                     planes[:].bitcast(I32)[32 * q + first_row : 32 * q + first_row + 4, 0 : columns // 4],
-                    picked[:].bitcast(I32)[32 * q : 32 * q + 32 : 8, :],
+                    picked[:].bitcast(I32)[32 * q : 32 * q + 32 : 8, start // 4 : (start + columns) // 4],
                 )
 
-        def deal_words(name, picked):
-            dealt = sb(name, [P, S], U32)
+        def deal_words(name, picked, tag=None):
+            dealt = sb(name, [P, S], U32, tag)
             nc.vector.tensor_copy(
                 dealt[:].bitcast(I32).rearrange("p (t a b) -> p a t b", t=PACK, b=4),
                 picked[:].bitcast(I32).rearrange("p (a b t) -> p a t b", t=PACK, b=4),
             )
             return dealt
 
-        def deal_bytes(name, planes):
-            dealt = sb(name, [P, S], U8)
+        def deal_bytes(name, planes, tag=None):
+            dealt = sb(name, [P, S], U8, tag)
             nc.vector.tensor_copy(
                 dealt[:].rearrange("p (t m) -> p t m", t=PACK),
                 planes[:, 0:S].rearrange("p (m t) -> p t m", t=PACK),
             )
             return dealt
 
-        x_w = load_words("x_w", x_words, T)
         x_sc = load_scale_rows("x_sc", x_scales, T)
         d_sc = load_scale_rows("d_sc", d_scales, G)
         offs_l = load_list("offs", offs)
@@ -86,40 +85,42 @@ def tile_picked_mtthzkcpswpagsn_none_po_kernel(
         k1_l = load_list("k1", k1)
         k2_l = load_list("k2", k2)
         k3_l = load_list("k3", k3)
+        x_w = load_words("x_w", x_words, T)
         d_w = load_words("d_w", d_words, G)
+        gs_sb = sb("gs", [P, PACK], F32)
+        nc.sync.dma_start(gs_sb[:], gs.rearrange("(p t) o -> p (t o)", t=PACK))
         cand_l = load_list("cand", cand)
         n2_l = load_list("n2", n2)
         n1_l = load_list("n1", n1)
         n3_l = load_list("n3", n3)
         n4_l = load_list("n4", n4)
         n5_l = load_list("n5", n5)
-        gs_sb = sb("gs", [P, PACK], F32)
-        nc.sync.dma_start(gs_sb[:], gs.rearrange("(p t) o -> p (t o)", t=PACK))
         n8_l = load_list("n8", n8)
         n6_l = load_list("n6", n6)
         n7_l = load_list("n7", n7)
 
-        planes = sb("planes", [P, 4 * S], U8)
+        planes = sb("planes", [P, 2 * S], U8)
         nc.vector.memset(planes[:].bitcast(I32), 0)
         cand_plane = sb("cand_plane", [P, S], U8)
         nc.vector.memset(cand_plane[:].bitcast(I32), 0)
+
+        LATE = 4 * S - 64
+        picked_sc = [sb("picked_sc%d" % j, [P, 2 * S], U8) for j in range(2)]
+        picked_sc.append(
+            shared.tile([P, 2 * S], U8, name="picked_sc2", tag="picked_sc2", align_bytes=64, offset=LATE)
+        )
+        gather(picked_sc[0][:, S : 2 * S], x_sc, offs_l[:])
+        gather(picked_sc[1][:, S : 2 * S], x_sc, two_l[:])
+        gather(picked_sc[2][:, S : 2 * S], x_sc, hz_l[:])
+        for j, held in enumerate((k1_l, k2_l, k3_l)):
+            gather(picked_sc[j][:, 0:S], d_sc, held[:])
+            place_scale_rows(planes, 4 * j, picked_sc[j], 0, 2 * S, (nc.sync, nc.scalar))
 
         mov = []
         for j, held in enumerate((offs_l, two_l)):
             picked = sb("xw%d" % j, [P, S], U32)
             gather(picked[:], x_w, held[:])
             mov.append(picked)
-
-        picked4 = sb("picked4", [P, 4 * S], U8)
-        for j, window, held in ((1, x_sc, offs_l), (2, x_sc, two_l), (3, x_sc, hz_l), (0, d_sc, k1_l)):
-            gather(picked4[:, j * S : (j + 1) * S], window, held[:])
-        place_scale_rows(planes, 0, picked4, 4 * S, (nc.sync, nc.scalar))
-        picked_k2 = sb("picked_k2", [P, S], U8)
-        gather(picked_k2[:], d_sc, k2_l[:])
-        place_scale_rows(planes, 4, picked_k2, S, (nc.sync, nc.scalar))
-        picked_k3 = shared.tile([P, S], U8, name="picked_k3", tag="picked_k3", align_bytes=64, offset=4 * S - S // 2)
-        gather(picked_k3[:], d_sc, k3_l[:])
-        place_scale_rows(planes, 8, picked_k3, S, (nc.sync, nc.scalar))
 
         dealt = []
         for j, held in enumerate((k1_l, k2_l, k3_l)):
@@ -143,36 +144,50 @@ def tile_picked_mtthzkcpswpagsn_none_po_kernel(
                     lhsT=dealt[j][:, cols].bitcast(FP8X4),
                     lhsT_scale=stat_scales[4 * j : P, cols],
                     rhs=mov[j][:].bitcast(FP8X4),
-                    rhs_scale=planes[:, (j + 1) * S : (j + 2) * S],
+                    rhs_scale=planes[4 * j : P, S : 2 * S],
                     start=(j == 0),
                     stop=(j == 2),
                 )
 
         picked_c = shared.tile([P, S], U8, name="picked_c", tag="picked_c", align_bytes=64, offset=4 * S)
         gather(picked_c[:], x_sc, cand_l[:])
-        place_scale_rows(cand_plane, 0, picked_c, S, (nc.sync,))
+        place_scale_rows(cand_plane, 0, picked_c, 0, S, (nc.sync,))
+        picked_cw = shared.tile([P, S], U32, name="picked_cw", tag="picked_cw", align_bytes=64, offset=5 * S)
+        gather(picked_cw[:], x_w, cand_l[:])
 
         HALF = S // 2
-        zb = [sb("zb%d" % c, [P, HALF, PACK], BF16) for c in range(2)]
-        h, pa, pb, ub, h5, diff = [], [], [], [], [], []
+        gain = sb("gain", [P, PACK, W], F32)
+        nc.scalar.copy(gain[:], gs_sb[:].unsqueeze(2).to_broadcast([P, PACK, W]))
+        neg_gs = sb("neg_gs", [P, PACK], F32)
+        nc.scalar.activation(neg_gs[:], gs_sb[:], COPY, scale=-1.0)
 
-        def fetch_pairs(t):
+        zb = [sb("zb%d" % c, [P, HALF, PACK], BF16) for c in range(2)]
+        z_low = sb("z_low", [P, 2, S], F32)
+        z_high = [sb("z_high%d" % c, [P, 2, HALF], F32) for c in range(2)]
+        h, ub, h5 = [], [], []
+        pa = [sb("pa%d" % u, [P, 2, W], F32) for u in range(2)]
+        pb = [sb("pb%d" % u, [P, 2, W], F32) for u in range(2)]
+
+        def fetch_b(t):
             h.append(sb("h%d" % t, [P, S], F32))
             nc.scalar.activation(h[t][:], banks[t][:], COPY, scale=SIXTEENTH)
-            pb.append(sb("pb%d" % t, [P, W], F32))
-            nc.scalar.activation(pb[t][:], h[t][:].indirect(n2_l[:]), COPY)
-            pa.append(sb("pa%d" % t, [P, W], F32))
-            nc.scalar.activation(pa[t][:], h[t][:].indirect(n1_l[:]), COPY)
+            nc.scalar.activation(pb[t // 2][:, t % 2, :], h[t][:].indirect(n2_l[:]), COPY)
 
-        def put_pairs(t):
+        def fetch_a(t):
+            nc.scalar.activation(pa[t // 2][:, t % 2, :], h[t][:].indirect(n1_l[:]), COPY)
+
+        def put_b(t):
             ub.append(sb("ub%d" % t, [P, S], F32))
-            nc.vector.tensor_copy(ub[t][:].indirect(n3_l[:]), pb[t][:])
-            rb = sb("rb%d" % t, [P, W], F32)
-            nc.vector.tensor_tensor(rb[:], pa[t][:], pb[t][:], ALU.max)
-            nc.vector.tensor_copy(ub[t][:].indirect(n4_l[:]), rb[:])
+            nc.vector.tensor_tensor(ub[t][:].indirect(n3_l[:]), pb[t // 2][:, t % 2, :], gain[:, t, :], ALU.mult)
+
+        def put_larger(u):
+            rb = sb("rb%d" % u, [P, 2, W], F32)
+            nc.vector.tensor_tensor(rb[:], pa[u][:], pb[u][:], ALU.max)
+            for t in (2 * u, 2 * u + 1):
+                nc.vector.tensor_tensor(ub[t][:].indirect(n4_l[:]), rb[:, t % 2, :], gain[:, t, :], ALU.mult)
 
         def fetch_n5(t):
-            h5.append(sb("h5_%d" % t, [P, S], F32))
+            h5.append(sb("h5_%d" % t, [P, S], F32, "xw%d" % t if t < 2 else None))
             for c in range(2):
                 nc.scalar.activation(
                     h5[t][:, c * HALF : (c + 1) * HALF],
@@ -181,40 +196,45 @@ def tile_picked_mtthzkcpswpagsn_none_po_kernel(
                 )
 
         def subtract(t):
-            diff.append(sb("diff%d" % t, [P, S], F32))
-            nc.vector.tensor_tensor(diff[t][:], ub[t][:], h5[t][:], ALU.subtract)
+            nc.vector.scalar_tensor_tensor(
+                z_low[:, t, :], h5[t][:], neg_gs[:, t : t + 1], ub[t][:], ALU.mult, ALU.add
+            )
 
-        def round_z(t):
-            for c in range(2):
-                nc.scalar.activation(
-                    zb[c][:, :, t], diff[t][:, c * HALF : (c + 1) * HALF], COPY, scale=gs_sb[:, t : t + 1]
-                )
+        def round_z(c, pair, source):
+            nc.scalar.copy(zb[c][:, :, 2 * pair : 2 * pair + 2], source.rearrange("p e n -> p n e"))
 
-        fetch_pairs(0)
-        put_pairs(0)
-        fetch_pairs(1)
+        fetch_b(0)
+        put_b(0)
+        fetch_b(1)
+        put_b(1)
+        fetch_a(0)
+        fetch_a(1)
+        put_larger(0)
+        fetch_b(2)
+        put_b(2)
+        fetch_b(3)
+        put_b(3)
         fetch_n5(0)
-        put_pairs(1)
         subtract(0)
-        fetch_pairs(2)
         fetch_n5(1)
-        put_pairs(2)
         subtract(1)
-        fetch_pairs(3)
-        round_z(0)
+        fetch_a(2)
+        fetch_a(3)
+        put_larger(1)
         fetch_n5(2)
-        cand_scales = deal_bytes("cand_scales", cand_plane)
-        put_pairs(3)
-        subtract(2)
         fetch_n5(3)
-        round_z(1)
-        round_z(2)
-        subtract(3)
-        round_z(3)
+        for c in range(2):
+            round_z(c, 0, z_low[:, :, c * HALF : (c + 1) * HALF])
+        for c in range(2):
+            cols = slice(c * HALF, (c + 1) * HALF)
+            for t in (2, 3):
+                nc.vector.scalar_tensor_tensor(
+                    z_high[c][:, t - 2, :], h5[t][:, cols], neg_gs[:, t : t + 1], ub[t][:, cols], ALU.mult, ALU.add
+                )
+            round_z(c, 1, z_high[c][:])
 
-        picked_cw = sb("picked_cw", [P, S], U32, tag="ub3")
-        gather(picked_cw[:], x_w, cand_l[:])
-        cand_words = deal_words("cand_words", picked_cw)
+        cand_scales = deal_bytes("cand_scales", cand_plane, "ub2")
+        cand_words = deal_words("cand_words", picked_cw, "ub3")
 
         z_words = sb("z_words", [P, S], U32)
         z_scales = sb("z_scales", [P, S], U8)
@@ -226,14 +246,14 @@ def tile_picked_mtthzkcpswpagsn_none_po_kernel(
                 in_=zb[c][:].rearrange("p n t -> p (n t)"),
             )
 
-        s = [sb("s%d" % t, [P, S], F32) for t in range(PACK)]
+        s_first = sb("s_first", [P, 2, S], F32)
+        s_last = sb("s_last", [P, 2, S], F32)
+        s = {2: s_first[:, 0, :], 0: s_first[:, 1, :], 1: s_last[:, 0, :], 3: s_last[:, 1, :]}
 
-        def score(t, cols, tag):
-            width = cols.stop - cols.start
-            bank = psum.tile([P, width], F32, name="sb_" + tag, tag=tag)
+        def product(out, t, cols):
             rows = slice(t * P, (t + 1) * P)
             nc.tensor.matmul_mx(
-                out=bank[:],
+                out=out,
                 lhsT=cand_words[:, rows].bitcast(FP8X4),
                 lhsT_scale=cand_scales[:, rows],
                 rhs=z_words[:, cols].bitcast(FP8X4),
@@ -241,11 +261,18 @@ def tile_picked_mtthzkcpswpagsn_none_po_kernel(
                 start=True,
                 stop=True,
             )
+
+        def score(t, cols, tag):
+            bank = psum.tile([P, cols.stop - cols.start], F32, name="sb_" + tag, tag=tag)
+            product(bank[:], t, cols)
             nc.scalar.activation(s[t][:, cols], bank[:], COPY, scale=SIXTEENTH)
 
         score(2, slice(0, HALF), "bank4")
-        score(2, slice(HALF, S), "bank5")
-        score(0, slice(0, S), "bank6")
+        score(0, slice(0, HALF), "bank5")
+        both = psum.tile([P, 2, HALF], F32, name="both", tag="bank6")
+        product(both[:, 0, :], 2, slice(HALF, S))
+        product(both[:, 1, :], 0, slice(HALF, S))
+        nc.scalar.activation(s_first[:, :, HALF:S], both[:], COPY, scale=SIXTEENTH)
         score(1, slice(0, S), "bank7")
         score(3, slice(0, S), "bank0")
 
@@ -254,19 +281,14 @@ def tile_picked_mtthzkcpswpagsn_none_po_kernel(
         out_rows = out_0.rearrange("(p t) n -> t p n", t=PACK)
         ds, up, page = {}, {}, {}
 
-        def send(t):
-            ds[t] = sb("ds%d" % t, [P, 2 * S], F32)
-            if t == 2:
-                for c in range(2):
-                    nc.vector.tensor_copy(
-                        ds[t][:].indirect(n8_l[:, c * 16 : (c + 1) * 16]), s[t][:, c * HALF : (c + 1) * HALF]
-                    )
-            else:
-                nc.vector.tensor_copy(ds[t][:].indirect(n8_l[:]), s[t][:])
+        def send(t, start, stop):
+            if start == 0:
+                ds[t] = sb("ds%d" % t, [P, 2 * S], F32)
+            nc.vector.tensor_copy(ds[t][:].indirect(n8_l[:, start // 16 : stop // 16]), s[t][:, start:stop])
 
         def larger(t):
             up[t] = sb("up%d" % t, [P, S], F32)
-            nc.vector.tensor_tensor(up[t][:], s[t][:], ds[t][:, 0:S], ALU.max)
+            nc.vector.tensor_tensor(up[t][:], s[t], ds[t][:, 0:S], ALU.max)
 
         def put_ds(t):
             page[t] = sb("page%d" % t, [P, U], F32, tag="page%d" % (t % 2 if t < 2 else 2))
@@ -281,16 +303,18 @@ def tile_picked_mtthzkcpswpagsn_none_po_kernel(
                 else:
                     nc.scalar.copy(ob[c][:, :, t], page[t][:, c * CH : (c + 1) * CH])
 
-        send(2)
-        send(0)
+        send(2, 0, HALF)
+        send(0, 0, HALF)
+        send(2, HALF, S)
+        send(0, HALF, S)
         larger(2)
         put_ds(2)
-        send(1)
-        put_up(2)
         larger(0)
         put_ds(0)
-        send(3)
+        put_up(2)
+        send(1, 0, S)
         put_up(0)
+        send(3, 0, S)
         larger(1)
         put_ds(1)
         larger(3)
@@ -308,8 +332,10 @@ def tile_picked_mtthzkcpswpagsn_none_po_kernel(
                 scales=o_scales[:, cols],
                 in_=ob[c][:].rearrange("p n t -> p (n t)"),
             )
-            nc.sync.dma_start(words_out[:, cols], o_words[:].bitcast(I32)[:, cols])
+            if c > 0:
+                ready = slice(0 if c == 1 else c * CH, (c + 1) * CH)
+                nc.sync.dma_start(words_out[:, ready], o_words[:].bitcast(I32)[:, ready])
         for q in range(4):
-            nc.sync.dma_start(
+            (nc.scalar if q < 3 else nc.sync).dma_start(
                 out_2[0].bitcast(I32)[4 * q : 4 * q + 4, :], o_scales[:].bitcast(I32)[32 * q : 32 * q + 4, :]
             )

from contextlib import ExitStack

import concourse.mybir as mybir

F32 = mybir.dt.float32
BF16 = mybir.dt.bfloat16
I32 = mybir.dt.int32
U32 = mybir.dt.uint32
U16 = mybir.dt.uint16
U8 = mybir.dt.uint8
FP8X4 = mybir.dt.float8_e4m3fn_x4
COPY = mybir.ActivationFunctionType.Copy
ALU = mybir.AluOpType

P = 128
PACK = 4
T, G, S, W, U = 1024, 2048, 512, 256, 1024
SIXTEENTH = 0.0625
FLOPS = 4 * 2 * 512 * 512 * 512


def tile_picked_mtthzkcpswpagsn_none_po_kernel(
    tc, x_words, x_scales, d_words, d_scales, gs, offs, k1, two, k2, hz, k3,
    n1, n2, n3, n4, n5, cand, n6, n7, n8, out_0, out_1, out_2,
):
    nc = tc.nc
    with ExitStack() as ctx:
        lists = ctx.enter_context(tc.tile_pool(name="lists", bufs=1))
        pool = ctx.enter_context(tc.tile_pool(name="work", bufs=1))
        shared = ctx.enter_context(tc.tile_pool(name="shared", bufs=1))
        psum = ctx.enter_context(tc.psum_pool(name="psum", bufs=1))

        def sb(name, shape, dtype, tag=None):
            return pool.tile(shape, dtype, name=name, tag=tag or name, align_bytes=64)

        def load_list(name, dram):
            held = lists.tile(list(dram.shape), U16, name=name, tag=name)
            nc.sync.dma_start(held[:], dram)
            return held

        def load_scale_rows(name, dram, columns):
            window = sb(name, [P, columns], U8)
            nc.gpsimd.memset(window[:].bitcast(I32), 0)
            nc.sync.dma_start(window[:].bitcast(I32)[0:P:8, :], dram[0].bitcast(I32))
            return window

        def load_words(name, dram, columns):
            window = sb(name, [P, columns], U32)
            nc.sync.dma_start(
                window[:].bitcast(I32), dram[0].rearrange("p n t -> p (n t)").bitcast(I32)
            )
            return window

        def gather(out, window, offsets):
            nc.vector.tensor_copy(out, window[:].indirect(offsets))

        def place_scale_rows(planes, first_row, picked, start, columns, queues):
            for q in range(4):
                queues[q % len(queues)].dma_start(
                    planes[:].bitcast(I32)[32 * q + first_row : 32 * q + first_row + 4, 0 : columns // 4],
                    picked[:].bitcast(I32)[32 * q : 32 * q + 32 : 8, start // 4 : (start + columns) // 4],
                )

        def deal_words(name, picked, tag=None):
            dealt = sb(name, [P, S], U32, tag)
            nc.vector.tensor_copy(
                dealt[:].bitcast(I32).rearrange("p (t a b) -> p a t b", t=PACK, b=4),
                picked[:].bitcast(I32).rearrange("p (a b t) -> p a t b", t=PACK, b=4),
            )
            return dealt

        def deal_bytes(name, planes, tag=None):
            dealt = sb(name, [P, S], U8, tag)
            nc.vector.tensor_copy(
                dealt[:].rearrange("p (t m) -> p t m", t=PACK),
                planes[:, 0:S].rearrange("p (m t) -> p t m", t=PACK),
            )
            return dealt

        x_sc = load_scale_rows("x_sc", x_scales, T)
        d_sc = load_scale_rows("d_sc", d_scales, G)
        offs_l = load_list("offs", offs)
        two_l = load_list("two", two)
        hz_l = load_list("hz", hz)
        k1_l = load_list("k1", k1)
        k2_l = load_list("k2", k2)
        k3_l = load_list("k3", k3)
        x_w = load_words("x_w", x_words, T)
        d_w = load_words("d_w", d_words, G)
        gs_sb = sb("gs", [P, PACK], F32)
        nc.sync.dma_start(gs_sb[:], gs.rearrange("(p t) o -> p (t o)", t=PACK))
        cand_l = load_list("cand", cand)
        n2_l = load_list("n2", n2)
        n1_l = load_list("n1", n1)
        n3_l = load_list("n3", n3)
        n4_l = load_list("n4", n4)
        n5_l = load_list("n5", n5)
        n8_l = load_list("n8", n8)
        n6_l = load_list("n6", n6)
        n7_l = load_list("n7", n7)

        planes = sb("planes", [P, 2 * S], U8)
        nc.vector.memset(planes[:].bitcast(I32), 0)
        cand_plane = sb("cand_plane", [P, S], U8)
        nc.vector.memset(cand_plane[:].bitcast(I32), 0)

        LATE = 4 * S - 64
        picked_sc = [sb("picked_sc%d" % j, [P, 2 * S], U8) for j in range(2)]
        picked_sc.append(
            shared.tile([P, 2 * S], U8, name="picked_sc2", tag="picked_sc2", align_bytes=64, offset=LATE)
        )
        gather(picked_sc[0][:, S : 2 * S], x_sc, offs_l[:])
        gather(picked_sc[1][:, S : 2 * S], x_sc, two_l[:])
        gather(picked_sc[2][:, S : 2 * S], x_sc, hz_l[:])
        for j, held in enumerate((k1_l, k2_l, k3_l)):
            gather(picked_sc[j][:, 0:S], d_sc, held[:])
            place_scale_rows(planes, 4 * j, picked_sc[j], 0, 2 * S, (nc.sync, nc.scalar))

        mov = []
        for j, held in enumerate((offs_l, two_l)):
            picked = sb("xw%d" % j, [P, S], U32)
            gather(picked[:], x_w, held[:])
            mov.append(picked)

        dealt = []
        for j, held in enumerate((k1_l, k2_l, k3_l)):
            picked = sb("kw%d" % j, [P, S], U32)
            gather(picked[:], d_w, held[:])
            if j > 0:
                dealt.append(deal_words("kd%d" % (j - 1), before))
            before = picked
        dealt.append(deal_words("kd2", before))
        stat_scales = deal_bytes("stat_scales", planes)
        picked = shared.tile([P, S], U32, name="xw2", tag="xw2", align_bytes=64, offset=0)
        gather(picked[:], x_w, hz_l[:])
        mov.append(picked)

        banks = [psum.tile([P, S], F32, name="hb%d" % t, tag="bank%d" % t) for t in range(PACK)]
        for t in range(PACK):
            for j in range(3):
                cols = slice(t * P, (t + 1) * P)
                nc.tensor.matmul_mx(
                    out=banks[t][:],
                    lhsT=dealt[j][:, cols].bitcast(FP8X4),
                    lhsT_scale=stat_scales[4 * j : P, cols],
                    rhs=mov[j][:].bitcast(FP8X4),
                    rhs_scale=planes[4 * j : P, S : 2 * S],
                    start=(j == 0),
                    stop=(j == 2),
                )

        picked_c = shared.tile([P, S], U8, name="picked_c", tag="picked_c", align_bytes=64, offset=4 * S)
        gather(picked_c[:], x_sc, cand_l[:])
        place_scale_rows(cand_plane, 0, picked_c, 0, S, (nc.sync,))
        picked_cw = shared.tile([P, S], U32, name="picked_cw", tag="picked_cw", align_bytes=64, offset=5 * S)
        gather(picked_cw[:], x_w, cand_l[:])

        HALF = S // 2
        gain = sb("gain", [P, PACK, W], F32)
        nc.scalar.copy(gain[:], gs_sb[:].unsqueeze(2).to_broadcast([P, PACK, W]))
        neg_gs = sb("neg_gs", [P, PACK], F32)
        nc.scalar.activation(neg_gs[:], gs_sb[:], COPY, scale=-1.0)

        zb = [sb("zb%d" % c, [P, HALF, PACK], BF16) for c in range(2)]
        z_low = sb("z_low", [P, 2, S], F32)
        z_high = [sb("z_high%d" % c, [P, 2, HALF], F32) for c in range(2)]
        h, ub, h5 = [], [], []
        pa = [sb("pa%d" % u, [P, 2, W], F32) for u in range(2)]
        pb = [sb("pb%d" % u, [P, 2, W], F32) for u in range(2)]

        def fetch_b(t):
            h.append(sb("h%d" % t, [P, S], F32))
            nc.scalar.activation(h[t][:], banks[t][:], COPY, scale=SIXTEENTH)
            nc.scalar.activation(pb[t // 2][:, t % 2, :], h[t][:].indirect(n2_l[:]), COPY)

        def fetch_a(t):
            nc.scalar.activation(pa[t // 2][:, t % 2, :], h[t][:].indirect(n1_l[:]), COPY)

        def put_b(t):
            ub.append(sb("ub%d" % t, [P, S], F32))
            nc.vector.tensor_tensor(ub[t][:].indirect(n3_l[:]), pb[t // 2][:, t % 2, :], gain[:, t, :], ALU.mult)

        def put_larger(u):
            rb = sb("rb%d" % u, [P, 2, W], F32)
            nc.vector.tensor_tensor(rb[:], pa[u][:], pb[u][:], ALU.max)
            for t in (2 * u, 2 * u + 1):
                nc.vector.tensor_tensor(ub[t][:].indirect(n4_l[:]), rb[:, t % 2, :], gain[:, t, :], ALU.mult)

        def fetch_n5(t):
            h5.append(sb("h5_%d" % t, [P, S], F32, "xw%d" % t if t < 2 else None))
            for c in range(2):
                nc.scalar.activation(
                    h5[t][:, c * HALF : (c + 1) * HALF],
                    h[t][:].indirect(n5_l[:, c * 16 : (c + 1) * 16]),
                    COPY,
                )

        def subtract(t):
            nc.vector.scalar_tensor_tensor(
                z_low[:, t, :], h5[t][:], neg_gs[:, t : t + 1], ub[t][:], ALU.mult, ALU.add
            )

        def round_z(c, pair, source):
            nc.scalar.copy(zb[c][:, :, 2 * pair : 2 * pair + 2], source.rearrange("p e n -> p n e"))

        fetch_b(0)
        put_b(0)
        fetch_b(1)
        put_b(1)
        fetch_a(0)
        fetch_a(1)
        put_larger(0)
        fetch_b(2)
        put_b(2)
        fetch_b(3)
        put_b(3)
        fetch_n5(0)
        subtract(0)
        fetch_n5(1)
        subtract(1)
        fetch_a(2)
        fetch_a(3)
        put_larger(1)
        fetch_n5(2)
        fetch_n5(3)
        for c in range(2):
            round_z(c, 0, z_low[:, :, c * HALF : (c + 1) * HALF])
        for c in range(2):
            cols = slice(c * HALF, (c + 1) * HALF)
            for t in (2, 3):
                nc.vector.scalar_tensor_tensor(
                    z_high[c][:, t - 2, :], h5[t][:, cols], neg_gs[:, t : t + 1], ub[t][:, cols], ALU.mult, ALU.add
                )
            round_z(c, 1, z_high[c][:])

        cand_scales = deal_bytes("cand_scales", cand_plane, "ub2")
        cand_words = deal_words("cand_words", picked_cw, "ub3")

        z_words = sb("z_words", [P, S], U32)
        z_scales = sb("z_scales", [P, S], U8)
        for c in range(2):
            cols = slice(c * HALF, (c + 1) * HALF)
            nc.vector.quantize_mx(
                out=z_words[:, cols].bitcast(FP8X4),
                scales=z_scales[:, cols],
                in_=zb[c][:].rearrange("p n t -> p (n t)"),
            )

        s_first = sb("s_first", [P, 2, S], F32)
        s_last = sb("s_last", [P, 2, S], F32)
        s = {2: s_first[:, 0, :], 0: s_first[:, 1, :], 1: s_last[:, 0, :], 3: s_last[:, 1, :]}

        def product(out, t, cols):
            rows = slice(t * P, (t + 1) * P)
            nc.tensor.matmul_mx(
                out=out,
                lhsT=cand_words[:, rows].bitcast(FP8X4),
                lhsT_scale=cand_scales[:, rows],
                rhs=z_words[:, cols].bitcast(FP8X4),
                rhs_scale=z_scales[:, cols],
                start=True,
                stop=True,
            )

        def score(t, cols, tag):
            bank = psum.tile([P, cols.stop - cols.start], F32, name="sb_" + tag, tag=tag)
            product(bank[:], t, cols)
            nc.scalar.activation(s[t][:, cols], bank[:], COPY, scale=SIXTEENTH)

        score(2, slice(0, HALF), "bank4")
        score(0, slice(0, HALF), "bank5")
        both = psum.tile([P, 2, HALF], F32, name="both", tag="bank6")
        product(both[:, 0, :], 2, slice(HALF, S))
        product(both[:, 1, :], 0, slice(HALF, S))
        nc.scalar.activation(s_first[:, :, HALF:S], both[:], COPY, scale=SIXTEENTH)
        score(1, slice(0, S), "bank7")
        score(3, slice(0, S), "bank0")

        CH = 256
        ob = [sb("ob%d" % c, [P, CH, PACK], BF16) for c in range(U // CH)]
        out_rows = out_0.rearrange("(p t) n -> t p n", t=PACK)
        ds, up, page = {}, {}, {}

        def send(t, start, stop):
            if start == 0:
                ds[t] = sb("ds%d" % t, [P, 2 * S], F32)
            nc.vector.tensor_copy(ds[t][:].indirect(n8_l[:, start // 16 : stop // 16]), s[t][:, start:stop])

        def larger(t):
            up[t] = sb("up%d" % t, [P, S], F32)
            nc.vector.tensor_tensor(up[t][:], s[t], ds[t][:, 0:S], ALU.max)

        def put_ds(t):
            page[t] = sb("page%d" % t, [P, U], F32, tag="page%d" % (t % 2 if t < 2 else 2))
            nc.vector.tensor_copy(page[t][:].indirect(n6_l[:]), ds[t][:, 0:S])

        def put_up(t):
            nc.vector.tensor_copy(page[t][:].indirect(n7_l[:]), up[t][:])
            nc.sync.dma_start(out_rows[t], page[t][:])
            for c in range(U // CH):
                if t == 3 and c < 2:
                    nc.vector.tensor_copy(ob[c][:, :, t], page[t][:, c * CH : (c + 1) * CH])
                else:
                    nc.scalar.copy(ob[c][:, :, t], page[t][:, c * CH : (c + 1) * CH])

        send(2, 0, HALF)
        send(0, 0, HALF)
        send(2, HALF, S)
        send(0, HALF, S)
        larger(2)
        put_ds(2)
        larger(0)
        put_ds(0)
        put_up(2)
        send(1, 0, S)
        put_up(0)
        send(3, 0, S)
        larger(1)
        put_ds(1)
        larger(3)
        put_up(1)
        put_ds(3)
        put_up(3)

        o_words = sb("o_words", [P, U], U32)
        o_scales = sb("o_scales", [P, U], U8)
        words_out = out_1[0].rearrange("p n t -> p (n t)").bitcast(I32)
        for c in range(U // CH):
            cols = slice(c * CH, (c + 1) * CH)
            nc.vector.quantize_mx(
                out=o_words[:, cols].bitcast(FP8X4),
                scales=o_scales[:, cols],
                in_=ob[c][:].rearrange("p n t -> p (n t)"),
            )
            if c > 0:
                ready = slice(0 if c == 1 else c * CH, (c + 1) * CH)
                nc.sync.dma_start(words_out[:, ready], o_words[:].bitcast(I32)[:, ready])
        for q in range(4):
            (nc.scalar if q < 3 else nc.sync).dma_start(
                out_2[0].bitcast(I32)[4 * q : 4 * q + 4, :], o_scales[:].bitcast(I32)[32 * q : 32 * q + 4, :]
            )
